import numpy as np
import ml_dtypes


def mxq(x, axis, fmt="e4m3"):
    dtype, down = {"e4m3": (ml_dtypes.float8_e4m3fn, 7), "e5m2": (ml_dtypes.float8_e5m2, 14)}[fmt]
    v = np.moveaxis(np.asarray(x, np.float32).astype(ml_dtypes.bfloat16).astype(np.float64), axis, -1)
    blocks = v.reshape(v.shape[:-1] + (-1, 32))
    amax = np.abs(blocks).max(-1, keepdims=True)
    byte = np.maximum(np.where(amax > 0, np.frexp(amax)[1] - 1 + 127, 0) - down, 1)
    scale = np.exp2(byte - 127.0)
    codes = (blocks / scale).astype(np.float32).astype(dtype).astype(np.float64)
    return np.moveaxis((codes * scale).reshape(v.shape), -1, axis)


WIDE = False


def mx_kscale(k, group=512):
    if not WIDE:
        return np.ones(k)
    levels = np.array([10, -10, 5, -5, 0])
    if group != 512:
        return np.exp2(np.random.permutation(np.resize(levels, k // group))).repeat(group)
    if k % 512:
        return np.exp2(np.random.permutation(np.resize(levels, k // 32))).repeat(32)
    a = np.empty((k // 512, 16))
    for p in range(k // 512):
        a[p, :8] = np.random.permutation(np.resize(levels, 8))
        for g in range(8):
            far = levels[np.abs(levels - a[p, g]) >= 10]
            a[p, g + 8] = far[np.random.randint(len(far))]
    return np.exp2(a.ravel()).repeat(32)


def f64(x):
    return np.asarray(x).astype(np.float64)


def gelu(v):
    return 0.5 * v * (1.0 + np.tanh(0.7978845608028654 * (v + 0.044715 * v ** 3)))


G, D, K, M, N = 2, 256, 512, 256, 512


def setup_inputs():
    n = np.random.standard_normal
    s = mx_kscale(D, 0)[:, None]
    u = mx_kscale(K)[:, None]
    return {
        "x": (n((G, D, N)) * s).astype(np.float32),
        "w1": (n((G, D, K)) / np.sqrt(D) / s).astype(np.float32),
        "hs": (np.random.uniform(0.5, 2.0, (G, K, 1)) * u).astype(np.float32),
        "w2": (n((G, K, M)) / np.sqrt(K) / u).astype(np.float32),
        "b": (0.5 * n((G, K, 1))).astype(np.float32),
        "r": n((G, M, N)).astype(np.float32),
    }


def reference(x, w1, hs, w2, b, r):
    xq = mxq(f64(x), 1, "e4m3")
    h = mxq(f64(w1), 1, "e4m3").transpose(0, 2, 1) @ xq
    h = h + f64(b)
    h = (gelu(h)) * f64(hs)
    y = mxq(f64(w2), 1, "e4m3").transpose(0, 2, 1) @ mxq(h, 1, "e4m3")
    y = y + f64(r)
    return y

@@ -1,0 +1,274 @@
+from contextlib import ExitStack
+
+import concourse.mybir as mybir
+
+G, D, K, M, N = 2, 256, 512, 256, 512
+FLOPS = 2 * G * (D * K * N + K * M * N)
+
+F32 = mybir.dt.float32
+BF16 = mybir.dt.bfloat16
+U32 = mybir.dt.uint32
+U8 = mybir.dt.uint8
+FP8X4 = mybir.dt.float8_e4m3fn_x4
+GELU = mybir.ActivationFunctionType.Gelu_apprx_tanh
+COPY = mybir.ActivationFunctionType.Copy
+MULT = mybir.AluOpType.mult
+ADD = mybir.AluOpType.add
+
+P = 128
+PACK = 4
+ROWS = D // PACK
+NT = 128
+HALF = 256
+RUN = 4
+
+
+def tile_rows_gmlp_gelu_bias_res_kernel(tc, x, w1, hs, w2, b, r, out):
+    nc = tc.nc
+    with ExitStack() as ctx:
+        sb = ctx.enter_context(tc.tile_pool(name="sb", bufs=1))
+        ps = ctx.enter_context(tc.psum_pool(name="ps", bufs=1))
+        ctx.enter_context(tc.manual_schedule())
+
+        def tile(name, shape, dtype):
+            return sb.tile(shape, dtype, name=name, align_bytes=64)
+
+        def operand(name, words):
+            return (
+                tile(name + "_bf", [P, PACK * words], BF16),
+                tile(name + "_codes", [P, words], U32),
+                tile(name + "_scales", [P, words], U8),
+            )
+
+        def copy(engine, dst, src):
+            if engine == "S":
+                nc.scalar.copy(out=dst, in_=src)
+            else:
+                nc.vector.tensor_copy(out=dst, in_=src)
+
+        def words_view(flat):
+            return flat.rearrange("p (c i t) -> p c t i", i=RUN, t=PACK)
+
+        def rows_view(rows):
+            return rows.rearrange("p t (c i) -> p c t i", i=RUN)
+
+        def quantize(op, first, words):
+            values, codes, scales = op
+            nc.vector.quantize_mx(
+                out=codes[:, first : first + words].bitcast(FP8X4),
+                scales=scales[:, first : first + words],
+                in_=values[:, PACK * first : PACK * (first + words)],
+            )
+
+        def product(dst, lhs, lhs_first, rhs, rhs_first, rows):
+            nc.tensor.matmul_mx(
+                out=dst,
+                lhsT=lhs[1][rows, lhs_first : lhs_first + P].bitcast(FP8X4),
+                lhsT_scale=lhs[2][rows, lhs_first : lhs_first + P],
+                rhs=rhs[1][rows, rhs_first : rhs_first + NT].bitcast(FP8X4),
+                rhs_scale=rhs[2][rows, rhs_first : rhs_first + NT],
+                start=True,
+                stop=True,
+            )
+
+        x_rows = x.rearrange("g (p j) n -> (g p) j n", j=PACK)
+        w1_rows = w1.rearrange("g (p j) k -> (g p) j k", j=PACK)
+
+        x_loads = [(0, 128), (128, 128), (256, 256)]
+        x_raw = [tile("x_raw%d" % i, [P, PACK, w], F32) for i, (c0, w) in enumerate(x_loads)]
+        x_op = [operand("x%d" % i, w) for i, (c0, w) in enumerate(x_loads)]
+        w1_raw = tile("w1_raw", [P, PACK, K], F32)
+        w1_op = [operand("w1_%d" % i, 2 * P) for i in range(2)]
+        w2_raw = [tile("w2_raw%d" % g, [P, PACK, M], F32) for g in range(G)]
+        w2_op = [operand("w2_%d" % g, M) for g in range(G)]
+        r_sb = [tile("r_sb%d" % g, [P, 2, N], F32) for g in range(G)]
+        b_sb = tile("b_sb", [P, G, 8], F32)
+        hs_sb = tile("hs_sb", [P, G, 8], F32)
+        z_bank = [[ps.tile([P, 512], F32, name="z%d_%d" % (g, i)) for i in range(2)] for g in range(G)]
+        y_bank = [[ps.tile([P, 2, HALF], F32, name="y%d_%d" % (g, i)) for i in range(2)] for g in range(G)]
+        y_sb = [[tile("y_sb%d_%d" % (g, i), [P, 2, HALF], F32) for i in range(2)] for g in range(G)]
+
+        units = [(0, 0, 128, 0, 2), (1, 0, 128, 0, 2), (0, 128, 128, 0, 4), (1, 128, 128, 0, 4), (0, 256, 256, 0, 2), (1, 256, 128, 1, 4), (1, 384, 128, 0, 4)]
+        act = [tile("act%d" % u, [P, PACK, w], F32) for u, (g, c0, w, bank, per_bank) in enumerate(units)]
+        h_op = [operand("h%d" % u, w) for u, (g, c0, w, bank, per_bank) in enumerate(units)]
+
+        def load_x(i):
+            c0, w = x_loads[i]
+            nc.sync.dma_start(out=x_raw[i][:], in_=x_rows[:, :, c0 : c0 + w])
+
+        def load_w1():
+            nc.sync.dma_start(out=w1_raw[:], in_=w1_rows)
+
+        def load_w2(g):
+            nc.sync.dma_start(out=w2_raw[g][:], in_=w2[g].rearrange("(p j) m -> p j m", j=PACK))
+
+        def load_r(g, c0=0, w=N):
+            nc.sync.dma_start(out=r_sb[g][:, :, c0 : c0 + w], in_=r[g].rearrange("(a p) n -> p a n", p=P)[:, :, c0 : c0 + w])
+
+        def load_small(dst, src):
+            nc.sync.dma_start(out=dst[:, :, 0:PACK], in_=src.rearrange("g (p t) o -> p g (t o)", t=PACK))
+
+        def warm():
+            seed = tile("seed", [P, 1], F32)
+            sink = tile("sink", [P, 1], F32)
+            nc.gpsimd.memset(seed[:], 0.0)
+            nc.scalar.activation(out=sink[:], in_=seed[:], func=GELU)
+
+        def lay_w1(engine, i, s0=0, s1=P):
+            src = w1_raw[:].rearrange("p j (s t) -> p s j t", t=PACK)[:, s0:s1, :, 2 * i : 2 * i + 2]
+            dst = w1_op[i][0][:].rearrange("p (t s j) -> p s j t", t=2, j=PACK)[:, s0:s1, :, :]
+            copy(engine, dst, src)
+
+        def lay_x(engine, i, c0=0, c1=None):
+            c1 = x_loads[i][1] if c1 is None else c1
+            copy(engine, words_view(x_op[i][0][:, PACK * c0 : PACK * c1]), rows_view(x_raw[i][:, :, c0:c1]))
+
+        def lay_w2(engine, g, c0=0, c1=M):
+            copy(engine, words_view(w2_op[g][0][:, PACK * c0 : PACK * c1]), rows_view(w2_raw[g][:, :, c0:c1]))
+
+        def q_w1(i, first=0, words=2 * P):
+            quantize(w1_op[i], first, words)
+
+        def q_x(i):
+            quantize(x_op[i], 0, x_loads[i][1])
+
+        def q_w2(g):
+            quantize(w2_op[g], 0, M)
+
+        def z_view(u, t):
+            g, c0, w, bank, per_bank = units[u]
+            return z_bank[g][(bank + t // per_bank) % 2][:, (t % per_bank) * w : (t % per_bank + 1) * w]
+
+        def mm1(u, slots):
+            g, c0, w, bank, per_bank = units[u]
+            rows = slice(ROWS * g, ROWS * (g + 1))
+            for t in slots:
+                for c in range(0, w, NT):
+                    i = [n for n, (l0, lw) in enumerate(x_loads) if l0 <= c0 + c < l0 + lw][0]
+                    product(z_view(u, t)[:, c : c + NT], w1_op[t // 2], (t % 2) * P, x_op[i], c0 + c - x_loads[i][0], rows)
+
+        def gelu(u, slots):
+            g = units[u][0]
+            for t in slots:
+                nc.scalar.activation(out=act[u][:, t, :], in_=z_view(u, t), func=GELU, bias=b_sb[:, g, t : t + 1])
+
+        def scale(u):
+            g, c0, w, bank, per_bank = units[u]
+            factor = hs_sb[:, g, 0:PACK].unsqueeze(1).unsqueeze(3).to_broadcast([P, w // RUN, PACK, RUN])
+            nc.vector.tensor_tensor(out=words_view(h_op[u][0][:]), in0=rows_view(act[u][:]), in1=factor, op=MULT)
+
+        scaled = {}
+
+        def sscale(u, slots):
+            g, c0, w, bank, per_bank = units[u]
+            if u not in scaled:
+                scaled[u] = tile("scaled%d" % u, [P, PACK, w], BF16)
+            for t in slots:
+                nc.scalar.activation(out=scaled[u][:, t, :], in_=act[u][:, t, :], func=COPY, scale=hs_sb[:, g, t : t + 1])
+
+        def lay_h(u):
+            nc.vector.tensor_copy(out=words_view(h_op[u][0][:]), in_=rows_view(scaled[u][:]))
+
+        def q_h(u):
+            quantize(h_op[u], 0, units[u][2])
+
+        def mm2(u):
+            g, c0, w, bank, per_bank = units[u]
+            for c in range(0, w, NT):
+                col = (c0 + c) % HALF
+                for a in range(2):
+                    product(y_bank[g][c0 // HALF][:, a, col : col + NT], w2_op[g], a * P, h_op[u], c, slice(0, P))
+
+        def add(g, c0, w):
+            half, col = c0 // HALF, c0 % HALF
+            nc.vector.tensor_tensor(
+                out=y_sb[g][half][:, :, col : col + w],
+                in0=y_bank[g][half][:, :, col : col + w],
+                in1=r_sb[g][:, :, c0 : c0 + w],
+                op=ADD,
+            )
+
+        def store(g, c0, w):
+            half, col = c0 // HALF, c0 % HALF
+            nc.sync.dma_start(
+                out=out[g].rearrange("(a p) n -> p a n", p=P)[:, :, c0 : c0 + w],
+                in_=y_sb[g][half][:, :, col : col + w],
+            )
+
+        warm()
+        load_w1()
+        lay_w1("V", 0)
+        load_x(0)
+        lay_x("V", 0)
+        q_w1(0, 0, 128)
+        load_x(1)
+        load_small(hs_sb, hs)
+        load_small(b_sb, b)
+        load_x(2)
+        lay_w1("S", 1)
+        q_x(0)
+        q_w1(0, 128, 128)
+        q_w1(1)
+        lay_x("S", 1)
+        mm1(0, [0, 1])
+        gelu(0, [0, 1])
+        mm1(0, [2, 3])
+        gelu(0, [2, 3])
+        q_x(1)
+        mm1(1, [0, 1])
+        scale(0)
+        load_w2(0)
+        mm1(1, [2, 3])
+        gelu(1, [0, 1])
+        mm1(2, [0, 1, 2, 3])
+        gelu(1, [2, 3])
+        lay_x("V", 2)
+        q_h(0)
+        gelu(2, [0, 1, 2, 3])
+        q_x(2)
+        scale(1)
+        load_r(0)
+        mm1(3, [0, 1, 2, 3])
+        gelu(3, [0, 1, 2, 3])
+        scale(2)
+        lay_w2("S", 0)
+        load_w2(1)
+        mm1(5, [0, 1, 2, 3])
+        scale(3)
+        q_h(1)
+        q_h(2)
+        mm1(6, [0, 1, 2, 3])
+        load_r(1)
+        q_w2(0)
+        gelu(5, [0, 1, 2, 3])
+        mm1(4, [0, 1, 2, 3])
+        lay_w2("V", 1, 0, 128)
+        q_h(3)
+        scale(5)
+        mm2(2)
+        lay_w2("S", 1, 128, 256)
+        mm2(0)
+        q_w2(1)
+        add(0, 0, 256)
+        gelu(4, [0, 1, 2, 3])
+        mm2(1)
+        scale(4)
+        q_h(5)
+        gelu(6, [0, 1, 2, 3])
+        mm2(3)
+        store(0, 0, 256)
+        mm2(5)
+        q_h(4)
+        add(1, 0, 256)
+        sscale(6, [0, 1, 2, 3])
+        lay_h(6)
+        mm2(4)
+        add(1, 256, 128)
+        q_h(6)
+        store(1, 0, 256)
+        mm2(6)
+        store(1, 256, 128)
+        add(0, 256, 256)
+        add(1, 384, 128)
+        store(0, 256, 256)
+        store(1, 384, 128)

@@ -20,7 +20,7 @@ PACK = 4
 ROWS = D // PACK
 NT = 128
 HALF = 256
-RUN = 4
+RUN = 2
 
 
 def tile_rows_gmlp_gelu_bias_res_kernel(tc, x, w1, hs, w2, b, r, out):
@@ -46,11 +46,11 @@ def tile_rows_gmlp_gelu_bias_res_kernel(tc, x, w1, hs, w2, b, r, out):
             else:
                 nc.vector.tensor_copy(out=dst, in_=src)
 
-        def words_view(flat):
-            return flat.rearrange("p (c i t) -> p c t i", i=RUN, t=PACK)
+        def words_view(flat, run=RUN):
+            return flat.rearrange("p (c i t) -> p c t i", i=run, t=PACK)
 
-        def rows_view(rows):
-            return rows.rearrange("p t (c i) -> p c t i", i=RUN)
+        def rows_view(rows, run=RUN):
+            return rows.rearrange("p t (c i) -> p c t i", i=run)
 
         def quantize(op, first, words):
             values, codes, scales = op
@@ -129,8 +129,8 @@ def tile_rows_gmlp_gelu_bias_res_kernel(tc, x, w1, hs, w2, b, r, out):
         def q_w1(i, first=0, words=2 * P):
             quantize(w1_op[i], first, words)
 
-        def q_x(i):
-            quantize(x_op[i], 0, x_loads[i][1])
+        def q_x(i, c0=0, w=None):
+            quantize(x_op[i], c0, w or x_loads[i][1])
 
         def q_w2(g):
             quantize(w2_op[g], 0, M)
@@ -167,7 +167,7 @@ def tile_rows_gmlp_gelu_bias_res_kernel(tc, x, w1, hs, w2, b, r, out):
                 nc.scalar.activation(out=scaled[u][:, t, :], in_=act[u][:, t, :], func=COPY, scale=hs_sb[:, g, t : t + 1])
 
         def lay_h(u):
-            nc.vector.tensor_copy(out=words_view(h_op[u][0][:]), in_=rows_view(scaled[u][:]))
+            nc.vector.tensor_copy(out=words_view(h_op[u][0][:], 4), in_=rows_view(scaled[u][:], 4))
 
         def q_h(u):
             quantize(h_op[u], 0, units[u][2])

@@ -16,259 +16,215 @@ MULT = mybir.AluOpType.mult
 ADD = mybir.AluOpType.add
 
 P = 128
-PACK = 4
-ROWS = D // PACK
-NT = 128
-HALF = 256
-RUN = 2
+SLOTS = 4
+ROWS = D // SLOTS
+M_TILES = M // P
+PASS_N = 128
+HALF = N // 2
+PAIR = 2
+PAD = 8
+
+X_PIECES = [(0, 128), (128, 128), (256, 256)]
+SPANS = [(0, 0, 128), (1, 0, 256), (0, 128, 256), (1, 256, 256), (0, 384, 128)]
 
 
 def tile_rows_gmlp_gelu_bias_res_kernel(tc, x, w1, hs, w2, b, r, out):
     nc = tc.nc
+    on_vector = nc.vector.tensor_copy
+    on_scalar = nc.scalar.copy
+
     with ExitStack() as ctx:
-        sb = ctx.enter_context(tc.tile_pool(name="sb", bufs=1))
-        ps = ctx.enter_context(tc.psum_pool(name="ps", bufs=1))
+        sbuf = ctx.enter_context(tc.tile_pool(name="sbuf", bufs=1))
+        psum = ctx.enter_context(tc.psum_pool(name="psum", bufs=1))
         ctx.enter_context(tc.manual_schedule())
 
         def tile(name, shape, dtype):
-            return sb.tile(shape, dtype, name=name, align_bytes=64)
+            return sbuf.tile(shape, dtype, name=name, align_bytes=64)
 
         def operand(name, words):
             return (
-                tile(name + "_bf", [P, PACK * words], BF16),
+                tile(name + "_values", [P, SLOTS * words], BF16),
                 tile(name + "_codes", [P, words], U32),
                 tile(name + "_scales", [P, words], U8),
             )
 
-        def copy(engine, dst, src):
-            if engine == "S":
-                nc.scalar.copy(out=dst, in_=src)
-            else:
-                nc.vector.tensor_copy(out=dst, in_=src)
+        x_raw = [tile("x_raw%d" % i, [P, SLOTS, width], F32) for i, (col0, width) in enumerate(X_PIECES)]
+        x_mx = [operand("x%d" % i, width) for i, (col0, width) in enumerate(X_PIECES)]
+        w1_raw = tile("w1_raw", [P, SLOTS, K], F32)
+        w1_mx = [operand("w1_pair%d" % i, PAIR * P) for i in range(SLOTS // PAIR)]
+        w2_raw = [tile("w2_raw%d" % g, [P, SLOTS, M], F32) for g in range(G)]
+        w2_mx = [operand("w2_group%d" % g, M) for g in range(G)]
+        r_sb = [tile("r_sb%d" % g, [P, M_TILES, N], F32) for g in range(G)]
+        b_sb = tile("b_sb", [P, G, PAD], F32)
+        hs_sb = tile("hs_sb", [P, G, PAD], F32)
+        act = [tile("act%d" % s, [P, SLOTS, width], F32) for s, (g, col0, width) in enumerate(SPANS)]
+        h_mx = [operand("h%d" % s, width) for s, (g, col0, width) in enumerate(SPANS)]
+        z_bank = [
+            [psum.tile([P, PAIR * HALF], F32, name="z%d_%d" % (g, i)) for i in range(SLOTS // PAIR)] for g in range(G)
+        ]
+        y_bank = [[psum.tile([P, M_TILES, HALF], F32, name="y%d_%d" % (g, i)) for i in range(N // HALF)] for g in range(G)]
 
-        def words_view(flat, run=RUN):
-            return flat.rearrange("p (c i t) -> p c t i", i=run, t=PACK)
+        def as_words(values, run):
+            return values.rearrange("p (c i t) -> p c t i", i=run, t=SLOTS)
 
-        def rows_view(rows, run=RUN):
+        def as_rows(rows, run):
             return rows.rearrange("p t (c i) -> p c t i", i=run)
 
-        def quantize(op, first, words):
-            values, codes, scales = op
-            nc.vector.quantize_mx(
-                out=codes[:, first : first + words].bitcast(FP8X4),
-                scales=scales[:, first : first + words],
-                in_=values[:, PACK * first : PACK * (first + words)],
-            )
+        def quantize(mx):
+            values, codes, scales = mx
+            nc.vector.quantize_mx(out=codes[:].bitcast(FP8X4), scales=scales[:], in_=values[:])
 
-        def product(dst, lhs, lhs_first, rhs, rhs_first, rows):
+        def product(dst, lhs, lhs_col, rhs, rhs_col, rows):
             nc.tensor.matmul_mx(
                 out=dst,
-                lhsT=lhs[1][rows, lhs_first : lhs_first + P].bitcast(FP8X4),
-                lhsT_scale=lhs[2][rows, lhs_first : lhs_first + P],
-                rhs=rhs[1][rows, rhs_first : rhs_first + NT].bitcast(FP8X4),
-                rhs_scale=rhs[2][rows, rhs_first : rhs_first + NT],
+                lhsT=lhs[1][rows, lhs_col : lhs_col + P].bitcast(FP8X4),
+                lhsT_scale=lhs[2][rows, lhs_col : lhs_col + P],
+                rhs=rhs[1][rows, rhs_col : rhs_col + PASS_N].bitcast(FP8X4),
+                rhs_scale=rhs[2][rows, rhs_col : rhs_col + PASS_N],
                 start=True,
                 stop=True,
             )
 
-        x_rows = x.rearrange("g (p j) n -> (g p) j n", j=PACK)
-        w1_rows = w1.rearrange("g (p j) k -> (g p) j k", j=PACK)
-
-        x_loads = [(0, 128), (128, 128), (256, 256)]
-        x_raw = [tile("x_raw%d" % i, [P, PACK, w], F32) for i, (c0, w) in enumerate(x_loads)]
-        x_op = [operand("x%d" % i, w) for i, (c0, w) in enumerate(x_loads)]
-        w1_raw = tile("w1_raw", [P, PACK, K], F32)
-        w1_op = [operand("w1_%d" % i, 2 * P) for i in range(2)]
-        w2_raw = [tile("w2_raw%d" % g, [P, PACK, M], F32) for g in range(G)]
-        w2_op = [operand("w2_%d" % g, M) for g in range(G)]
-        r_sb = [tile("r_sb%d" % g, [P, 2, N], F32) for g in range(G)]
-        b_sb = tile("b_sb", [P, G, 8], F32)
-        hs_sb = tile("hs_sb", [P, G, 8], F32)
-        z_bank = [[ps.tile([P, 512], F32, name="z%d_%d" % (g, i)) for i in range(2)] for g in range(G)]
-        y_bank = [[ps.tile([P, 2, HALF], F32, name="y%d_%d" % (g, i)) for i in range(2)] for g in range(G)]
-        y_sb = [[tile("y_sb%d_%d" % (g, i), [P, 2, HALF], F32) for i in range(2)] for g in range(G)]
-
-        units = [(0, 0, 128, 0, 2), (1, 0, 128, 0, 2), (0, 128, 128, 0, 4), (1, 128, 128, 0, 4), (0, 256, 256, 0, 2), (1, 256, 128, 1, 4), (1, 384, 128, 0, 4)]
-        act = [tile("act%d" % u, [P, PACK, w], F32) for u, (g, c0, w, bank, per_bank) in enumerate(units)]
-        h_op = [operand("h%d" % u, w) for u, (g, c0, w, bank, per_bank) in enumerate(units)]
-
         def load_x(i):
-            c0, w = x_loads[i]
-            nc.sync.dma_start(out=x_raw[i][:], in_=x_rows[:, :, c0 : c0 + w])
+            col0, width = X_PIECES[i]
+            rows = x.rearrange("g (p t) n -> (g p) t n", t=SLOTS)
+            nc.sync.dma_start(out=x_raw[i][:], in_=rows[:, :, col0 : col0 + width])
 
-        def load_w1():
-            nc.sync.dma_start(out=w1_raw[:], in_=w1_rows)
+        def load_per_hidden(dst, src):
+            nc.sync.dma_start(out=dst[:, :, 0:SLOTS], in_=src.rearrange("g (p t) o -> p g (t o)", t=SLOTS))
 
         def load_w2(g):
-            nc.sync.dma_start(out=w2_raw[g][:], in_=w2[g].rearrange("(p j) m -> p j m", j=PACK))
+            nc.sync.dma_start(out=w2_raw[g][:], in_=w2[g].rearrange("(p t) m -> p t m", t=SLOTS))
 
-        def load_r(g, c0=0, w=N):
-            nc.sync.dma_start(out=r_sb[g][:, :, c0 : c0 + w], in_=r[g].rearrange("(a p) n -> p a n", p=P)[:, :, c0 : c0 + w])
+        def load_r(g):
+            nc.sync.dma_start(out=r_sb[g][:], in_=r[g].rearrange("(a p) n -> p a n", p=P))
 
-        def load_small(dst, src):
-            nc.sync.dma_start(out=dst[:, :, 0:PACK], in_=src.rearrange("g (p t) o -> p g (t o)", t=PACK))
+        def lay_w1(copy, i):
+            src = w1_raw[:].rearrange("p j (s t) -> p s j t", t=SLOTS)[:, :, :, PAIR * i : PAIR * (i + 1)]
+            copy(out=w1_mx[i][0][:].rearrange("p (t s j) -> p s j t", t=PAIR, j=SLOTS), in_=src)
 
-        def warm():
-            seed = tile("seed", [P, 1], F32)
-            sink = tile("sink", [P, 1], F32)
-            nc.gpsimd.memset(seed[:], 0.0)
-            nc.scalar.activation(out=sink[:], in_=seed[:], func=GELU)
+        def lay_x(copy, i):
+            copy(out=as_words(x_mx[i][0][:], 2), in_=as_rows(x_raw[i][:], 2))
 
-        def lay_w1(engine, i, s0=0, s1=P):
-            src = w1_raw[:].rearrange("p j (s t) -> p s j t", t=PACK)[:, s0:s1, :, 2 * i : 2 * i + 2]
-            dst = w1_op[i][0][:].rearrange("p (t s j) -> p s j t", t=2, j=PACK)[:, s0:s1, :, :]
-            copy(engine, dst, src)
+        def lay_w2(copy, g, col0, col1):
+            copy(out=as_words(w2_mx[g][0][:, SLOTS * col0 : SLOTS * col1], 2), in_=as_rows(w2_raw[g][:, :, col0:col1], 2))
 
-        def lay_x(engine, i, c0=0, c1=None):
-            c1 = x_loads[i][1] if c1 is None else c1
-            copy(engine, words_view(x_op[i][0][:, PACK * c0 : PACK * c1]), rows_view(x_raw[i][:, :, c0:c1]))
+        def z_view(s, t):
+            g, col0, width = SPANS[s]
+            return z_bank[g][t // PAIR][:, (t % PAIR) * width : (t % PAIR + 1) * width]
 
-        def lay_w2(engine, g, c0=0, c1=M):
-            copy(engine, words_view(w2_op[g][0][:, PACK * c0 : PACK * c1]), rows_view(w2_raw[g][:, :, c0:c1]))
+        def first_product(s):
+            g, col0, width = SPANS[s]
+            for t in range(SLOTS):
+                for c in range(0, width, PASS_N):
+                    i = max(n for n, piece in enumerate(X_PIECES) if piece[0] <= col0 + c)
+                    product(
+                        z_view(s, t)[:, c : c + PASS_N],
+                        w1_mx[t // PAIR],
+                        (t % PAIR) * P,
+                        x_mx[i],
+                        col0 + c - X_PIECES[i][0],
+                        slice(ROWS * g, ROWS * (g + 1)),
+                    )
 
-        def q_w1(i, first=0, words=2 * P):
-            quantize(w1_op[i], first, words)
+        def gelu(s):
+            g = SPANS[s][0]
+            for t in range(SLOTS):
+                nc.scalar.activation(out=act[s][:, t, :], in_=z_view(s, t), func=GELU, bias=b_sb[:, g, t : t + 1])
 
-        def q_x(i, c0=0, w=None):
-            quantize(x_op[i], c0, w or x_loads[i][1])
+        def scale_on_vector(s):
+            g, col0, width = SPANS[s]
+            factor = hs_sb[:, g, 0:SLOTS].unsqueeze(1).unsqueeze(3).to_broadcast([P, width // 2, SLOTS, 2])
+            nc.vector.tensor_tensor(out=as_words(h_mx[s][0][:], 2), in0=as_rows(act[s][:], 2), in1=factor, op=MULT)
 
-        def q_w2(g):
-            quantize(w2_op[g], 0, M)
+        def scale_on_scalar(s):
+            g, col0, width = SPANS[s]
+            h_rows = tile("h_rows%d" % s, [P, SLOTS, width], BF16)
+            for t in range(SLOTS):
+                nc.scalar.activation(out=h_rows[:, t, :], in_=act[s][:, t, :], func=COPY, scale=hs_sb[:, g, t : t + 1])
+            return h_rows
 
-        def z_view(u, t):
-            g, c0, w, bank, per_bank = units[u]
-            return z_bank[g][(bank + t // per_bank) % 2][:, (t % per_bank) * w : (t % per_bank + 1) * w]
+        def lay_h(s, h_rows):
+            nc.vector.tensor_copy(out=as_words(h_mx[s][0][:], 4), in_=as_rows(h_rows[:], 4))
 
-        def mm1(u, slots):
-            g, c0, w, bank, per_bank = units[u]
-            rows = slice(ROWS * g, ROWS * (g + 1))
-            for t in slots:
-                for c in range(0, w, NT):
-                    i = [n for n, (l0, lw) in enumerate(x_loads) if l0 <= c0 + c < l0 + lw][0]
-                    product(z_view(u, t)[:, c : c + NT], w1_op[t // 2], (t % 2) * P, x_op[i], c0 + c - x_loads[i][0], rows)
+        def second_product(s):
+            g, col0, width = SPANS[s]
+            for c in range(0, width, PASS_N):
+                half, col = divmod(col0 + c, HALF)
+                for a in range(M_TILES):
+                    product(y_bank[g][half][:, a, col : col + PASS_N], w2_mx[g], a * P, h_mx[s], c, slice(0, P))
 
-        def gelu(u, slots):
-            g = units[u][0]
-            for t in slots:
-                nc.scalar.activation(out=act[u][:, t, :], in_=z_view(u, t), func=GELU, bias=b_sb[:, g, t : t + 1])
-
-        def scale(u):
-            g, c0, w, bank, per_bank = units[u]
-            factor = hs_sb[:, g, 0:PACK].unsqueeze(1).unsqueeze(3).to_broadcast([P, w // RUN, PACK, RUN])
-            nc.vector.tensor_tensor(out=words_view(h_op[u][0][:]), in0=rows_view(act[u][:]), in1=factor, op=MULT)
-
-        scaled = {}
-
-        def sscale(u, slots):
-            g, c0, w, bank, per_bank = units[u]
-            if u not in scaled:
-                scaled[u] = tile("scaled%d" % u, [P, PACK, w], BF16)
-            for t in slots:
-                nc.scalar.activation(out=scaled[u][:, t, :], in_=act[u][:, t, :], func=COPY, scale=hs_sb[:, g, t : t + 1])
-
-        def lay_h(u):
-            nc.vector.tensor_copy(out=words_view(h_op[u][0][:], 4), in_=rows_view(scaled[u][:], 4))
-
-        def q_h(u):
-            quantize(h_op[u], 0, units[u][2])
-
-        def mm2(u):
-            g, c0, w, bank, per_bank = units[u]
-            for c in range(0, w, NT):
-                col = (c0 + c) % HALF
-                for a in range(2):
-                    product(y_bank[g][c0 // HALF][:, a, col : col + NT], w2_op[g], a * P, h_op[u], c, slice(0, P))
-
-        def add(g, c0, w):
-            half, col = c0 // HALF, c0 % HALF
+        def add_and_store(g, col0, width):
+            half, col = divmod(col0, HALF)
+            result = tile("result%d_%d" % (g, col0), [P, M_TILES, width], F32)
             nc.vector.tensor_tensor(
-                out=y_sb[g][half][:, :, col : col + w],
-                in0=y_bank[g][half][:, :, col : col + w],
-                in1=r_sb[g][:, :, c0 : c0 + w],
+                out=result[:],
+                in0=y_bank[g][half][:, :, col : col + width],
+                in1=r_sb[g][:, :, col0 : col0 + width],
                 op=ADD,
             )
+            rows = out[g].rearrange("(a p) n -> p a n", p=P)
+            nc.sync.dma_start(out=rows[:, :, col0 : col0 + width], in_=result[:])
 
-        def store(g, c0, w):
-            half, col = c0 // HALF, c0 % HALF
-            nc.sync.dma_start(
-                out=out[g].rearrange("(a p) n -> p a n", p=P)[:, :, c0 : c0 + w],
-                in_=y_sb[g][half][:, :, col : col + w],
-            )
+        seed = tile("seed", [P, 1], F32)
+        sink = tile("sink", [P, 1], F32)
+        nc.gpsimd.memset(seed[:], 0.0)
+        nc.scalar.activation(out=sink[:], in_=seed[:], func=GELU)
 
-        warm()
-        load_w1()
-        lay_w1("V", 0)
+        nc.sync.dma_start(out=w1_raw[:], in_=w1.rearrange("g (p j) k -> (g p) j k", j=SLOTS))
         load_x(0)
-        lay_x("V", 0)
-        q_w1(0, 0, 128)
         load_x(1)
-        load_small(hs_sb, hs)
-        load_small(b_sb, b)
+        load_per_hidden(b_sb, b)
         load_x(2)
-        lay_w1("S", 1)
-        q_x(0)
-        q_w1(0, 128, 128)
-        q_w1(1)
-        lay_x("S", 1)
-        mm1(0, [0, 1])
-        gelu(0, [0, 1])
-        mm1(0, [2, 3])
-        gelu(0, [2, 3])
-        q_x(1)
-        mm1(1, [0, 1])
-        scale(0)
-        load_w2(0)
-        mm1(1, [2, 3])
-        gelu(1, [0, 1])
-        mm1(2, [0, 1, 2, 3])
-        gelu(1, [2, 3])
-        lay_x("V", 2)
-        q_h(0)
-        gelu(2, [0, 1, 2, 3])
-        q_x(2)
-        scale(1)
-        load_r(0)
-        mm1(3, [0, 1, 2, 3])
-        gelu(3, [0, 1, 2, 3])
-        scale(2)
-        lay_w2("S", 0)
+        load_per_hidden(hs_sb, hs)
         load_w2(1)
-        mm1(5, [0, 1, 2, 3])
-        scale(3)
-        q_h(1)
-        q_h(2)
-        mm1(6, [0, 1, 2, 3])
+        load_w2(0)
         load_r(1)
-        q_w2(0)
-        gelu(5, [0, 1, 2, 3])
-        mm1(4, [0, 1, 2, 3])
-        lay_w2("V", 1, 0, 128)
-        q_h(3)
-        scale(5)
-        mm2(2)
-        lay_w2("S", 1, 128, 256)
-        mm2(0)
-        q_w2(1)
-        add(0, 0, 256)
-        gelu(4, [0, 1, 2, 3])
-        mm2(1)
-        scale(4)
-        q_h(5)
-        gelu(6, [0, 1, 2, 3])
-        mm2(3)
-        store(0, 0, 256)
-        mm2(5)
-        q_h(4)
-        add(1, 0, 256)
-        sscale(6, [0, 1, 2, 3])
-        lay_h(6)
-        mm2(4)
-        add(1, 256, 128)
-        q_h(6)
-        store(1, 0, 256)
-        mm2(6)
-        store(1, 256, 128)
-        add(0, 256, 256)
-        add(1, 384, 128)
-        store(0, 256, 256)
-        store(1, 384, 128)
+        load_r(0)
+
+        lay_w1(on_vector, 0)
+        lay_w1(on_scalar, 1)
+        lay_x(on_vector, 0)
+        quantize(w1_mx[0])
+        quantize(x_mx[0])
+        quantize(w1_mx[1])
+        first_product(0)
+        lay_x(on_scalar, 1)
+        quantize(x_mx[1])
+        first_product(1)
+        gelu(0)
+        lay_x(on_vector, 2)
+        scale_on_vector(0)
+        quantize(x_mx[2])
+        gelu(1)
+        first_product(2)
+        first_product(3)
+        quantize(h_mx[0])
+        lay_w2(on_vector, 1, 0, P)
+        lay_w2(on_scalar, 1, P, M)
+        scale_on_vector(1)
+        quantize(w2_mx[1])
+        quantize(h_mx[1])
+        gelu(2)
+        first_product(4)
+        second_product(1)
+        scale_on_vector(2)
+        lay_w2(on_scalar, 0, 0, M)
+        add_and_store(1, 0, HALF)
+        quantize(h_mx[2])
+        quantize(w2_mx[0])
+        second_product(0)
+        second_product(2)
+        gelu(3)
+        scale_on_vector(3)
+        gelu(4)
+        h_rows = scale_on_scalar(4)
+        add_and_store(0, 0, HALF)
+        quantize(h_mx[3])
+        second_product(3)
+        lay_h(4, h_rows)
+        add_and_store(0, 256, 128)
+        quantize(h_mx[4])
+        second_product(4)
+        add_and_store(1, HALF, HALF)
+        add_and_store(0, 384, 128)

@@ -19,13 +19,12 @@ P = 128
 SLOTS = 4
 ROWS = D // SLOTS
 M_TILES = M // P
-PASS_N = 128
-HALF = N // 2
+CHUNK = 128
+CHUNKS = N // CHUNK
 PAIR = 2
 PAD = 8
-
-X_PIECES = [(0, 128), (128, 128), (256, 256)]
-SPANS = [(0, 0, 128), (1, 0, 256), (0, 128, 256), (1, 256, 256), (0, 384, 128)]
+RUN_F32 = 2
+RUN_BF16 = 4
 
 
 def tile_rows_gmlp_gelu_bias_res_kernel(tc, x, w1, hs, w2, b, r, out):
@@ -48,8 +47,8 @@ def tile_rows_gmlp_gelu_bias_res_kernel(tc, x, w1, hs, w2, b, r, out):
                 tile(name + "_scales", [P, words], U8),
             )
 
-        x_raw = [tile("x_raw%d" % i, [P, SLOTS, width], F32) for i, (col0, width) in enumerate(X_PIECES)]
-        x_mx = [operand("x%d" % i, width) for i, (col0, width) in enumerate(X_PIECES)]
+        x_raw = [tile("x_raw%d" % c, [P, SLOTS, CHUNK], F32) for c in range(CHUNKS)]
+        x_mx = [operand("x%d" % c, CHUNK) for c in range(CHUNKS)]
         w1_raw = tile("w1_raw", [P, SLOTS, K], F32)
         w1_mx = [operand("w1_pair%d" % i, PAIR * P) for i in range(SLOTS // PAIR)]
         w2_raw = [tile("w2_raw%d" % g, [P, SLOTS, M], F32) for g in range(G)]
@@ -57,12 +56,13 @@ def tile_rows_gmlp_gelu_bias_res_kernel(tc, x, w1, hs, w2, b, r, out):
         r_sb = [tile("r_sb%d" % g, [P, M_TILES, N], F32) for g in range(G)]
         b_sb = tile("b_sb", [P, G, PAD], F32)
         hs_sb = tile("hs_sb", [P, G, PAD], F32)
-        act = [tile("act%d" % s, [P, SLOTS, width], F32) for s, (g, col0, width) in enumerate(SPANS)]
-        h_mx = [operand("h%d" % s, width) for s, (g, col0, width) in enumerate(SPANS)]
-        z_bank = [
-            [psum.tile([P, PAIR * HALF], F32, name="z%d_%d" % (g, i)) for i in range(SLOTS // PAIR)] for g in range(G)
+        act = [[tile("act%d_%d" % (g, c), [P, SLOTS, CHUNK], F32) for c in range(CHUNKS)] for g in range(G)]
+        h_mx = [[operand("h%d_%d" % (g, i), PAIR * CHUNK) for i in range(CHUNKS // PAIR)] for g in range(G)]
+        z_bank = [[psum.tile([P, SLOTS, CHUNK], F32, name="z%d_%d" % (g, i)) for i in range(2)] for g in range(G)]
+        y_bank = [
+            [psum.tile([P, M_TILES, PAIR * CHUNK], F32, name="y%d_%d" % (g, i)) for i in range(CHUNKS // PAIR)]
+            for g in range(G)
         ]
-        y_bank = [[psum.tile([P, M_TILES, HALF], F32, name="y%d_%d" % (g, i)) for i in range(N // HALF)] for g in range(G)]
 
         def as_words(values, run):
             return values.rearrange("p (c i t) -> p c t i", i=run, t=SLOTS)
@@ -70,101 +70,104 @@ def tile_rows_gmlp_gelu_bias_res_kernel(tc, x, w1, hs, w2, b, r, out):
         def as_rows(rows, run):
             return rows.rearrange("p t (c i) -> p c t i", i=run)
 
-        def quantize(mx):
+        def quantize(mx, first, words):
             values, codes, scales = mx
-            nc.vector.quantize_mx(out=codes[:].bitcast(FP8X4), scales=scales[:], in_=values[:])
+            nc.vector.quantize_mx(
+                out=codes[:, first : first + words].bitcast(FP8X4),
+                scales=scales[:, first : first + words],
+                in_=values[:, SLOTS * first : SLOTS * (first + words)],
+            )
 
         def product(dst, lhs, lhs_col, rhs, rhs_col, rows):
             nc.tensor.matmul_mx(
                 out=dst,
                 lhsT=lhs[1][rows, lhs_col : lhs_col + P].bitcast(FP8X4),
                 lhsT_scale=lhs[2][rows, lhs_col : lhs_col + P],
-                rhs=rhs[1][rows, rhs_col : rhs_col + PASS_N].bitcast(FP8X4),
-                rhs_scale=rhs[2][rows, rhs_col : rhs_col + PASS_N],
+                rhs=rhs[1][rows, rhs_col : rhs_col + CHUNK].bitcast(FP8X4),
+                rhs_scale=rhs[2][rows, rhs_col : rhs_col + CHUNK],
                 start=True,
                 stop=True,
             )
 
-        def load_x(i):
-            col0, width = X_PIECES[i]
+        def load_x(c):
             rows = x.rearrange("g (p t) n -> (g p) t n", t=SLOTS)
-            nc.sync.dma_start(out=x_raw[i][:], in_=rows[:, :, col0 : col0 + width])
+            nc.sync.dma_start(out=x_raw[c][:], in_=rows[:, :, c * CHUNK : (c + 1) * CHUNK])
 
         def load_per_hidden(dst, src):
             nc.sync.dma_start(out=dst[:, :, 0:SLOTS], in_=src.rearrange("g (p t) o -> p g (t o)", t=SLOTS))
-
-        def load_w2(g):
-            nc.sync.dma_start(out=w2_raw[g][:], in_=w2[g].rearrange("(p t) m -> p t m", t=SLOTS))
-
-        def load_r(g):
-            nc.sync.dma_start(out=r_sb[g][:], in_=r[g].rearrange("(a p) n -> p a n", p=P))
 
         def lay_w1(copy, i):
             src = w1_raw[:].rearrange("p j (s t) -> p s j t", t=SLOTS)[:, :, :, PAIR * i : PAIR * (i + 1)]
             copy(out=w1_mx[i][0][:].rearrange("p (t s j) -> p s j t", t=PAIR, j=SLOTS), in_=src)
 
-        def lay_x(copy, i):
-            copy(out=as_words(x_mx[i][0][:], 2), in_=as_rows(x_raw[i][:], 2))
+        def quantize_w1(t):
+            quantize(w1_mx[t // PAIR], (t % PAIR) * P, P)
+
+        def lay_x(c):
+            on_vector(out=as_words(x_mx[c][0][:], RUN_F32), in_=as_rows(x_raw[c][:], RUN_F32))
+
+        def quantize_x(c):
+            quantize(x_mx[c], 0, CHUNK)
 
         def lay_w2(copy, g, col0, col1):
-            copy(out=as_words(w2_mx[g][0][:, SLOTS * col0 : SLOTS * col1], 2), in_=as_rows(w2_raw[g][:, :, col0:col1], 2))
+            dst = w2_mx[g][0][:, SLOTS * col0 : SLOTS * col1]
+            copy(out=as_words(dst, RUN_F32), in_=as_rows(w2_raw[g][:, :, col0:col1], RUN_F32))
 
-        def z_view(s, t):
-            g, col0, width = SPANS[s]
-            return z_bank[g][t // PAIR][:, (t % PAIR) * width : (t % PAIR + 1) * width]
+        def quantize_w2(g):
+            quantize(w2_mx[g], 0, M)
 
-        def first_product(s):
-            g, col0, width = SPANS[s]
+        def z_view(g, c, t):
+            if c == 0:
+                return z_bank[g][t // PAIR][:, t % PAIR, :]
+            return z_bank[g][(c + 1) % 2][:, t, :]
+
+        def first_product(g, c):
             for t in range(SLOTS):
-                for c in range(0, width, PASS_N):
-                    i = max(n for n, piece in enumerate(X_PIECES) if piece[0] <= col0 + c)
-                    product(
-                        z_view(s, t)[:, c : c + PASS_N],
-                        w1_mx[t // PAIR],
-                        (t % PAIR) * P,
-                        x_mx[i],
-                        col0 + c - X_PIECES[i][0],
-                        slice(ROWS * g, ROWS * (g + 1)),
-                    )
+                rows = slice(ROWS * g, ROWS * (g + 1))
+                product(z_view(g, c, t), w1_mx[t // PAIR], (t % PAIR) * P, x_mx[c], 0, rows)
 
-        def gelu(s):
-            g = SPANS[s][0]
+        def gelu(g, c):
             for t in range(SLOTS):
-                nc.scalar.activation(out=act[s][:, t, :], in_=z_view(s, t), func=GELU, bias=b_sb[:, g, t : t + 1])
+                nc.scalar.activation(out=act[g][c][:, t, :], in_=z_view(g, c, t), func=GELU, bias=b_sb[:, g, t : t + 1])
 
-        def scale_on_vector(s):
-            g, col0, width = SPANS[s]
-            factor = hs_sb[:, g, 0:SLOTS].unsqueeze(1).unsqueeze(3).to_broadcast([P, width // 2, SLOTS, 2])
-            nc.vector.tensor_tensor(out=as_words(h_mx[s][0][:], 2), in0=as_rows(act[s][:], 2), in1=factor, op=MULT)
+        def h_values(g, c):
+            first = SLOTS * CHUNK * (c % PAIR)
+            return h_mx[g][c // PAIR][0][:, first : first + SLOTS * CHUNK]
 
-        def scale_on_scalar(s):
-            g, col0, width = SPANS[s]
-            h_rows = tile("h_rows%d" % s, [P, SLOTS, width], BF16)
+        def scale_on_vector(g, c):
+            factor = hs_sb[:, g, 0:SLOTS].unsqueeze(1).unsqueeze(3).to_broadcast([P, CHUNK // RUN_F32, SLOTS, RUN_F32])
+            nc.vector.tensor_tensor(
+                out=as_words(h_values(g, c), RUN_F32), in0=as_rows(act[g][c][:], RUN_F32), in1=factor, op=MULT
+            )
+
+        def scale_on_scalar(g, c):
+            h_rows = tile("h_rows", [P, SLOTS, CHUNK], BF16)
             for t in range(SLOTS):
-                nc.scalar.activation(out=h_rows[:, t, :], in_=act[s][:, t, :], func=COPY, scale=hs_sb[:, g, t : t + 1])
+                nc.scalar.activation(
+                    out=h_rows[:, t, :], in_=act[g][c][:, t, :], func=COPY, scale=hs_sb[:, g, t : t + 1]
+                )
             return h_rows
 
-        def lay_h(s, h_rows):
-            nc.vector.tensor_copy(out=as_words(h_mx[s][0][:], 4), in_=as_rows(h_rows[:], 4))
+        def lay_h(g, c, h_rows):
+            on_vector(out=as_words(h_values(g, c), RUN_BF16), in_=as_rows(h_rows[:], RUN_BF16))
 
-        def second_product(s):
-            g, col0, width = SPANS[s]
-            for c in range(0, width, PASS_N):
-                half, col = divmod(col0 + c, HALF)
+        def quantize_h(g, c, chunks):
+            quantize(h_mx[g][c // PAIR], (c % PAIR) * CHUNK, chunks * CHUNK)
+
+        def second_product(g, c, chunks):
+            for col in range((c % PAIR) * CHUNK, (c % PAIR + chunks) * CHUNK, CHUNK):
                 for a in range(M_TILES):
-                    product(y_bank[g][half][:, a, col : col + PASS_N], w2_mx[g], a * P, h_mx[s], c, slice(0, P))
+                    dst = y_bank[g][c // PAIR][:, a, col : col + CHUNK]
+                    product(dst, w2_mx[g], a * P, h_mx[g][c // PAIR], col, slice(0, P))
 
-        def add_and_store(g, col0, width):
-            half, col = divmod(col0, HALF)
-            result = tile("result%d_%d" % (g, col0), [P, M_TILES, width], F32)
+        def add_and_store(g, c, chunks):
+            col, width = (c % PAIR) * CHUNK, chunks * CHUNK
+            cols = slice(c * CHUNK, c * CHUNK + width)
+            result = tile("result%d_%d" % (g, c), [P, M_TILES, width], F32)
             nc.vector.tensor_tensor(
-                out=result[:],
-                in0=y_bank[g][half][:, :, col : col + width],
-                in1=r_sb[g][:, :, col0 : col0 + width],
-                op=ADD,
+                out=result[:], in0=y_bank[g][c // PAIR][:, :, col : col + width], in1=r_sb[g][:, :, cols], op=ADD
             )
-            rows = out[g].rearrange("(a p) n -> p a n", p=P)
-            nc.sync.dma_start(out=rows[:, :, col0 : col0 + width], in_=result[:])
+            nc.sync.dma_start(out=out[g].rearrange("(a p) n -> p a n", p=P)[:, :, cols], in_=result[:])
 
         seed = tile("seed", [P, 1], F32)
         sink = tile("sink", [P, 1], F32)
@@ -177,54 +180,68 @@ def tile_rows_gmlp_gelu_bias_res_kernel(tc, x, w1, hs, w2, b, r, out):
         load_per_hidden(b_sb, b)
         load_x(2)
         load_per_hidden(hs_sb, hs)
-        load_w2(1)
-        load_w2(0)
-        load_r(1)
-        load_r(0)
+        load_x(3)
+        for g in range(G):
+            nc.sync.dma_start(out=w2_raw[g][:], in_=w2[g].rearrange("(p t) m -> p t m", t=SLOTS))
+        for g in range(G):
+            nc.sync.dma_start(out=r_sb[g][:], in_=r[g].rearrange("(a p) n -> p a n", p=P))
 
         lay_w1(on_vector, 0)
         lay_w1(on_scalar, 1)
-        lay_x(on_vector, 0)
-        quantize(w1_mx[0])
-        quantize(x_mx[0])
-        quantize(w1_mx[1])
-        first_product(0)
-        lay_x(on_scalar, 1)
-        quantize(x_mx[1])
-        first_product(1)
-        gelu(0)
-        lay_x(on_vector, 2)
-        scale_on_vector(0)
-        quantize(x_mx[2])
-        gelu(1)
-        first_product(2)
-        first_product(3)
-        quantize(h_mx[0])
-        lay_w2(on_vector, 1, 0, P)
-        lay_w2(on_scalar, 1, P, M)
-        scale_on_vector(1)
-        quantize(w2_mx[1])
-        quantize(h_mx[1])
-        gelu(2)
-        first_product(4)
-        second_product(1)
-        scale_on_vector(2)
+        lay_x(0)
+        quantize_w1(0)
+        quantize_x(0)
+        quantize_w1(1)
+        quantize_w1(2)
+        quantize_w1(3)
+        first_product(0, 0)
+        first_product(1, 0)
+        lay_x(1)
+        quantize_x(1)
+        gelu(0, 0)
+        first_product(0, 1)
+        lay_x(2)
+        scale_on_vector(0, 0)
+        quantize_x(2)
+        gelu(1, 0)
+        first_product(1, 1)
+        first_product(0, 2)
+        first_product(1, 2)
+        scale_on_vector(1, 0)
+        lay_x(3)
+        gelu(0, 1)
+        scale_on_vector(0, 1)
+        quantize_x(3)
+        gelu(1, 1)
+        first_product(0, 3)
+        first_product(1, 3)
+        quantize_h(0, 0, 2)
+        scale_on_vector(1, 1)
         lay_w2(on_scalar, 0, 0, M)
-        add_and_store(1, 0, HALF)
-        quantize(h_mx[2])
-        quantize(w2_mx[0])
-        second_product(0)
-        second_product(2)
-        gelu(3)
-        scale_on_vector(3)
-        gelu(4)
-        h_rows = scale_on_scalar(4)
-        add_and_store(0, 0, HALF)
-        quantize(h_mx[3])
-        second_product(3)
-        lay_h(4, h_rows)
-        add_and_store(0, 256, 128)
-        quantize(h_mx[4])
-        second_product(4)
-        add_and_store(1, HALF, HALF)
-        add_and_store(0, 384, 128)
+        lay_w2(on_vector, 1, 0, P)
+        quantize_w2(0)
+        second_product(0, 0, 2)
+        quantize_h(1, 0, 2)
+        gelu(0, 2)
+        scale_on_vector(0, 2)
+        lay_w2(on_scalar, 1, P, M)
+        quantize_w2(1)
+        second_product(1, 0, 2)
+        add_and_store(0, 0, 2)
+        gelu(1, 2)
+        scale_on_vector(1, 2)
+        gelu(0, 3)
+        scale_on_vector(0, 3)
+        quantize_h(1, 2, 1)
+        second_product(1, 2, 1)
+        quantize_h(0, 2, 2)
+        second_product(0, 2, 2)
+        add_and_store(1, 0, 2)
+        gelu(1, 3)
+        h_rows = scale_on_scalar(1, 3)
+        lay_h(1, 3, h_rows)
+        add_and_store(1, 2, 1)
+        quantize_h(1, 3, 1)
+        second_product(1, 3, 1)
+        add_and_store(0, 2, 2)
+        add_and_store(1, 3, 1)

from contextlib import ExitStack

import concourse.mybir as mybir

G, D, K, M, N = 2, 256, 512, 256, 512
FLOPS = 2 * G * (D * K * N + K * M * N)

F32 = mybir.dt.float32
BF16 = mybir.dt.bfloat16
U32 = mybir.dt.uint32
U8 = mybir.dt.uint8
FP8X4 = mybir.dt.float8_e4m3fn_x4
GELU = mybir.ActivationFunctionType.Gelu_apprx_tanh
COPY = mybir.ActivationFunctionType.Copy
MULT = mybir.AluOpType.mult
ADD = mybir.AluOpType.add

P = 128
SLOTS = 4
ROWS = D // SLOTS
M_TILES = M // P
CHUNK = 128
CHUNKS = N // CHUNK
PAIR = 2
PAD = 8
RUN_F32 = 2
RUN_BF16 = 4


def tile_rows_gmlp_gelu_bias_res_kernel(tc, x, w1, hs, w2, b, r, out):
    nc = tc.nc
    on_vector = nc.vector.tensor_copy
    on_scalar = nc.scalar.copy

    with ExitStack() as ctx:
        sbuf = ctx.enter_context(tc.tile_pool(name="sbuf", bufs=1))
        psum = ctx.enter_context(tc.psum_pool(name="psum", bufs=1))
        ctx.enter_context(tc.manual_schedule())

        def tile(name, shape, dtype):
            return sbuf.tile(shape, dtype, name=name, align_bytes=64)

        def operand(name, words):
            return (
                tile(name + "_values", [P, SLOTS * words], BF16),
                tile(name + "_codes", [P, words], U32),
                tile(name + "_scales", [P, words], U8),
            )

        x_raw = [tile("x_raw%d" % c, [P, SLOTS, CHUNK], F32) for c in range(CHUNKS)]
        x_mx = [operand("x%d" % c, CHUNK) for c in range(CHUNKS)]
        w1_raw = tile("w1_raw", [P, SLOTS, K], F32)
        w1_mx = [operand("w1_pair%d" % i, PAIR * P) for i in range(SLOTS // PAIR)]
        w2_raw = [tile("w2_raw%d" % g, [P, SLOTS, M], F32) for g in range(G)]
        w2_mx = [operand("w2_group%d" % g, M) for g in range(G)]
        r_sb = [tile("r_sb%d" % g, [P, M_TILES, N], F32) for g in range(G)]
        b_sb = tile("b_sb", [P, G, PAD], F32)
        hs_sb = tile("hs_sb", [P, G, PAD], F32)
        act = [[tile("act%d_%d" % (g, c), [P, SLOTS, CHUNK], F32) for c in range(CHUNKS)] for g in range(G)]
        h_mx = [[operand("h%d_%d" % (g, i), PAIR * CHUNK) for i in range(CHUNKS // PAIR)] for g in range(G)]
        z_bank = [[psum.tile([P, SLOTS, CHUNK], F32, name="z%d_%d" % (g, i)) for i in range(2)] for g in range(G)]
        y_bank = [
            [psum.tile([P, M_TILES, PAIR * CHUNK], F32, name="y%d_%d" % (g, i)) for i in range(CHUNKS // PAIR)]
            for g in range(G)
        ]

        def as_words(values, run):
            return values.rearrange("p (c i t) -> p c t i", i=run, t=SLOTS)

        def as_rows(rows, run):
            return rows.rearrange("p t (c i) -> p c t i", i=run)

        def quantize(mx, first, words):
            values, codes, scales = mx
            nc.vector.quantize_mx(
                out=codes[:, first : first + words].bitcast(FP8X4),
                scales=scales[:, first : first + words],
                in_=values[:, SLOTS * first : SLOTS * (first + words)],
            )

        def product(dst, lhs, lhs_col, rhs, rhs_col, rows):
            nc.tensor.matmul_mx(
                out=dst,
                lhsT=lhs[1][rows, lhs_col : lhs_col + P].bitcast(FP8X4),
                lhsT_scale=lhs[2][rows, lhs_col : lhs_col + P],
                rhs=rhs[1][rows, rhs_col : rhs_col + CHUNK].bitcast(FP8X4),
                rhs_scale=rhs[2][rows, rhs_col : rhs_col + CHUNK],
                start=True,
                stop=True,
            )

        def load_x(c):
            rows = x.rearrange("g (p t) n -> (g p) t n", t=SLOTS)
            nc.sync.dma_start(out=x_raw[c][:], in_=rows[:, :, c * CHUNK : (c + 1) * CHUNK])

        def load_per_hidden(dst, src):
            nc.sync.dma_start(out=dst[:, :, 0:SLOTS], in_=src.rearrange("g (p t) o -> p g (t o)", t=SLOTS))

        def lay_w1(copy, i):
            src = w1_raw[:].rearrange("p j (s t) -> p s j t", t=SLOTS)[:, :, :, PAIR * i : PAIR * (i + 1)]
            copy(out=w1_mx[i][0][:].rearrange("p (t s j) -> p s j t", t=PAIR, j=SLOTS), in_=src)

        def quantize_w1(t):
            quantize(w1_mx[t // PAIR], (t % PAIR) * P, P)

        def lay_x(c):
            on_vector(out=as_words(x_mx[c][0][:], RUN_F32), in_=as_rows(x_raw[c][:], RUN_F32))

        def quantize_x(c):
            quantize(x_mx[c], 0, CHUNK)

        def lay_w2(copy, g, col0, col1):
            dst = w2_mx[g][0][:, SLOTS * col0 : SLOTS * col1]
            copy(out=as_words(dst, RUN_F32), in_=as_rows(w2_raw[g][:, :, col0:col1], RUN_F32))

        def quantize_w2(g):
            quantize(w2_mx[g], 0, M)

        def z_view(g, c, t):
            if c == 0:
                return z_bank[g][t // PAIR][:, t % PAIR, :]
            return z_bank[g][(c + 1) % 2][:, t, :]

        def first_product(g, c):
            for t in range(SLOTS):
                rows = slice(ROWS * g, ROWS * (g + 1))
                product(z_view(g, c, t), w1_mx[t // PAIR], (t % PAIR) * P, x_mx[c], 0, rows)

        def gelu(g, c):
            for t in range(SLOTS):
                nc.scalar.activation(out=act[g][c][:, t, :], in_=z_view(g, c, t), func=GELU, bias=b_sb[:, g, t : t + 1])

        def h_values(g, c):
            first = SLOTS * CHUNK * (c % PAIR)
            return h_mx[g][c // PAIR][0][:, first : first + SLOTS * CHUNK]

        def scale_on_vector(g, c):
            factor = hs_sb[:, g, 0:SLOTS].unsqueeze(1).unsqueeze(3).to_broadcast([P, CHUNK // RUN_F32, SLOTS, RUN_F32])
            nc.vector.tensor_tensor(
                out=as_words(h_values(g, c), RUN_F32), in0=as_rows(act[g][c][:], RUN_F32), in1=factor, op=MULT
            )

        def scale_on_scalar(g, c):
            h_rows = tile("h_rows", [P, SLOTS, CHUNK], BF16)
            for t in range(SLOTS):
                nc.scalar.activation(
                    out=h_rows[:, t, :], in_=act[g][c][:, t, :], func=COPY, scale=hs_sb[:, g, t : t + 1]
                )
            return h_rows

        def lay_h(g, c, h_rows):
            on_vector(out=as_words(h_values(g, c), RUN_BF16), in_=as_rows(h_rows[:], RUN_BF16))

        def quantize_h(g, c, chunks):
            quantize(h_mx[g][c // PAIR], (c % PAIR) * CHUNK, chunks * CHUNK)

        def second_product(g, c, chunks):
            for col in range((c % PAIR) * CHUNK, (c % PAIR + chunks) * CHUNK, CHUNK):
                for a in range(M_TILES):
                    dst = y_bank[g][c // PAIR][:, a, col : col + CHUNK]
                    product(dst, w2_mx[g], a * P, h_mx[g][c // PAIR], col, slice(0, P))

        def add_and_store(g, c, chunks):
            col, width = (c % PAIR) * CHUNK, chunks * CHUNK
            cols = slice(c * CHUNK, c * CHUNK + width)
            result = tile("result%d_%d" % (g, c), [P, M_TILES, width], F32)
            nc.vector.tensor_tensor(
                out=result[:], in0=y_bank[g][c // PAIR][:, :, col : col + width], in1=r_sb[g][:, :, cols], op=ADD
            )
            nc.sync.dma_start(out=out[g].rearrange("(a p) n -> p a n", p=P)[:, :, cols], in_=result[:])

        seed = tile("seed", [P, 1], F32)
        sink = tile("sink", [P, 1], F32)
        nc.gpsimd.memset(seed[:], 0.0)
        nc.scalar.activation(out=sink[:], in_=seed[:], func=GELU)

        nc.sync.dma_start(out=w1_raw[:], in_=w1.rearrange("g (p j) k -> (g p) j k", j=SLOTS))
        load_x(0)
        load_x(1)
        load_per_hidden(b_sb, b)
        load_x(2)
        load_per_hidden(hs_sb, hs)
        load_x(3)
        for g in range(G):
            nc.sync.dma_start(out=w2_raw[g][:], in_=w2[g].rearrange("(p t) m -> p t m", t=SLOTS))
        for g in range(G):
            nc.sync.dma_start(out=r_sb[g][:], in_=r[g].rearrange("(a p) n -> p a n", p=P))

        lay_w1(on_vector, 0)
        lay_w1(on_scalar, 1)
        lay_x(0)
        quantize_w1(0)
        quantize_x(0)
        quantize_w1(1)
        quantize_w1(2)
        quantize_w1(3)
        first_product(0, 0)
        first_product(1, 0)
        lay_x(1)
        quantize_x(1)
        gelu(0, 0)
        first_product(0, 1)
        lay_x(2)
        scale_on_vector(0, 0)
        quantize_x(2)
        gelu(1, 0)
        first_product(1, 1)
        first_product(0, 2)
        first_product(1, 2)
        scale_on_vector(1, 0)
        lay_x(3)
        gelu(0, 1)
        scale_on_vector(0, 1)
        quantize_x(3)
        gelu(1, 1)
        first_product(0, 3)
        first_product(1, 3)
        quantize_h(0, 0, 2)
        scale_on_vector(1, 1)
        lay_w2(on_scalar, 0, 0, M)
        lay_w2(on_vector, 1, 0, P)
        quantize_w2(0)
        second_product(0, 0, 2)
        quantize_h(1, 0, 2)
        gelu(0, 2)
        scale_on_vector(0, 2)
        lay_w2(on_scalar, 1, P, M)
        quantize_w2(1)
        second_product(1, 0, 2)
        add_and_store(0, 0, 2)
        gelu(1, 2)
        scale_on_vector(1, 2)
        gelu(0, 3)
        scale_on_vector(0, 3)
        quantize_h(1, 2, 1)
        second_product(1, 2, 1)
        quantize_h(0, 2, 2)
        second_product(0, 2, 2)
        add_and_store(1, 0, 2)
        gelu(1, 3)
        h_rows = scale_on_scalar(1, 3)
        lay_h(1, 3, h_rows)
        add_and_store(1, 2, 1)
        quantize_h(1, 3, 1)
        second_product(1, 3, 1)
        add_and_store(0, 2, 2)
        add_and_store(1, 3, 1)
